import numpy as np
import ml_dtypes


def mxq(x, axis, fmt="e4m3"):
    dtype, down = {"e4m3": (ml_dtypes.float8_e4m3fn, 7), "e5m2": (ml_dtypes.float8_e5m2, 14)}[fmt]
    v = np.moveaxis(np.asarray(x, np.float32).astype(ml_dtypes.bfloat16).astype(np.float64), axis, -1)
    blocks = v.reshape(v.shape[:-1] + (-1, 32))
    amax = np.abs(blocks).max(-1, keepdims=True)
    byte = np.maximum(np.where(amax > 0, np.frexp(amax)[1] - 1 + 127, 0) - down, 1)
    scale = np.exp2(byte - 127.0)
    codes = (blocks / scale).astype(np.float32).astype(dtype).astype(np.float64)
    return np.moveaxis((codes * scale).reshape(v.shape), -1, axis)


WIDE = False


def mx_kscale(k):
    if not WIDE:
        return np.ones(k)
    levels = np.array([10, -10, 5, -5, 0])
    if k % 512:
        return np.exp2(np.random.permutation(np.resize(levels, k // 32))).repeat(32)
    a = np.empty((k // 512, 16))
    for p in range(k // 512):
        a[p, :8] = np.random.permutation(np.resize(levels, 8))
        for g in range(8):
            far = levels[np.abs(levels - a[p, g]) >= 10]
            a[p, g + 8] = far[np.random.randint(len(far))]
    return np.exp2(a.ravel()).repeat(32)


def f64(x):
    return np.asarray(x).astype(np.float64)


def striped(idx):
    return np.tile(idx.reshape(-1, 16).T, (8, 1)).astype(np.uint16)


def unstriped(offs):
    return offs[:16].T.reshape(-1).astype(np.int64)


E2M1 = np.array([0.0, 0.5, 1.0, 1.5, 2.0, 3.0, 4.0, 6.0, -0.0, -0.5, -1.0, -1.5, -2.0, -3.0, -4.0, -6.0])


def pack_weight(w, fmt):
    k, n = w.shape
    w = f64(np.asarray(w, np.float32).astype(ml_dtypes.bfloat16)).reshape(k // 32, 32, n)
    amax = np.abs(w).max(1)
    if fmt == "e4m3":
        byte = np.frexp(amax)[1] - 1 + 127 - 7
    else:
        mant, ex = np.frexp(amax / 6.0)
        byte = np.where(mant > 0.5, ex, ex - 1) + 127
    byte = np.clip(np.where(amax > 0, byte, 1), 1, 254)
    scaled = (w * np.exp2(127.0 - byte)[:, None, :]).reshape(k, n).astype(np.float32)
    by_word = np.ascontiguousarray(scaled.reshape(k // 512, 128, 4, n).transpose(0, 1, 3, 2))
    if fmt == "e4m3":
        words = by_word.astype(ml_dtypes.float8_e4m3fn).view(np.uint8)
    else:
        c = by_word.astype(ml_dtypes.float4_e2m1fn).view(np.uint8) & 0xF
        words = (c[..., 0::2] | (c[..., 1::2] << 4)).reshape(k // 512, 128, 2 * n)
    return np.ascontiguousarray(words), np.ascontiguousarray(byte.astype(np.uint8).reshape(k // 512, 16, n))


def unpack_weight(words, scales, fmt):
    g, _, n = scales.shape
    words = np.ascontiguousarray(words).reshape(g, 128, n, -1)
    if fmt == "e4m3":
        vals = words.view(ml_dtypes.float8_e4m3fn).astype(np.float64)
    else:
        nib = np.empty((g, 128, n, 4), np.uint8)
        nib[..., 0::2] = words & 0xF
        nib[..., 1::2] = words >> 4
        vals = E2M1[nib]
    vals = vals * np.repeat(np.exp2(scales.astype(np.float64) - 127.0), 8, axis=1)[..., None]
    return vals.transpose(0, 1, 3, 2).reshape(g * 512, n)


K, T, E, C, N = 1536, 512, 4, 256, 512
M = 512


def by_expert(wq, xq):
    return np.concatenate([wq[e].T @ xq[:, e * C:(e + 1) * C] for e in range(E)], axis=1)


def setup_inputs():
    n = np.random.standard_normal
    s = mx_kscale(K)[:, None]
    v = mx_kscale(N)
    first = np.random.permutation(np.repeat(np.arange(E), T // E))
    second = (first + 1 + np.random.permutation(np.repeat(np.arange(E - 1), -(-T // (E - 1)))[:T])) % E
    while np.bincount(second, minlength=E).max() != T // E:
        load = np.bincount(second, minlength=E); hi, lo = int(load.argmax()), int(load.argmin())
        t = np.flatnonzero((second == hi) & (first != lo))[0]; second[t] = lo
    slot_token = np.empty(E * C, np.int64); pos = np.empty((2, T), np.int64); fill = np.zeros(E, np.int64)
    place = np.stack([np.random.permutation(C) for _ in range(E)])
    for r, deal in enumerate((first, second)):
        for t in np.random.permutation(T):
            e = deal[t]; j = e * C + place[e, fill[e]]; fill[e] += 1; slot_token[j] = t; pos[r, t] = j
    g = np.random.uniform(0.2, 0.8, T)
    x = pack_weight(n((K, T)) * s, "e4m3")
    return {
        "x_words": x[0],
        "x_scales": x[1],
        "w": (n((E, K, N)) / np.sqrt(K) / s[None] * v[None, None, :]).astype(np.float32),
        "b": (0.3 * n((N, E)) * v[:, None]).astype(np.float32),
        "wp": (n((N, M)) / np.sqrt(N) / v[:, None]).astype(np.float32),
        "gate": np.stack([np.tile(g, (N, 1)), np.tile(1.0 - g, (N, 1))]).astype(np.float32),
        "offs": striped(slot_token),
        "pos1": striped(pos[0]),
        "pos2": striped(pos[1]),
    }


def reference(x_words, x_scales, w, b, wp, gate, offs, pos1, pos2):
    idx = unstriped(offs)
    xq = unpack_weight(x_words, x_scales, "e4m3")[:, idx]
    y = by_expert(mxq(f64(w), 1, "e4m3"), xq)
    y = y + np.repeat(f64(b), C, axis=1)
    c = f64(gate[0]) * y[:, unstriped(pos1)] + f64(gate[1]) * y[:, unstriped(pos2)]
    return mxq(f64(wp), 0, "e4m3").T @ mxq(c, 0, "e4m3")

@@ -1,0 +1,242 @@
+from contextlib import ExitStack
+
+import concourse.mybir as mybir
+from concourse.masks import make_identity
+
+K, T, E, C, N, M = 1536, 512, 4, 256, 512, 512
+S = E * C
+FLOPS = 2 * K * N * S + 2 * N * M * T
+
+F32 = mybir.dt.float32
+BF16 = mybir.dt.bfloat16
+I32 = mybir.dt.int32
+U32 = mybir.dt.uint32
+U16 = mybir.dt.uint16
+U8 = mybir.dt.uint8
+FP8X4 = mybir.dt.float8_e4m3fn_x4
+ACT = mybir.ActivationFunctionType
+ALU = mybir.AluOpType
+
+P = 128
+PACK = 4
+KP = P * PACK
+PASSES = K // KP
+HALF = N // 2
+VECTOR_CASTS = (11, 21, 22, 23)
+FREE_GATHERS = 7
+Y_AFTER = (9, 10, 17, 18)
+PICK_AFTER = (None, 14, 16, 19)
+FIRST_AFTER = 22
+
+
+def tile_moe_nxt_lin_bias_kernel(
+    tc, x_words, x_scales, w, b, wp, gate, offs, pos1, pos2, out
+):
+    nc = tc.nc
+    with ExitStack() as ctx:
+        keep = ctx.enter_context(tc.tile_pool(name="keep", bufs=1))
+        ring = ctx.enter_context(tc.tile_pool(name="ring", bufs=8))
+        psum = ctx.enter_context(tc.psum_pool(name="psum", bufs=1))
+
+        def bank(i, shape):
+            return psum.tile(shape, F32, tag=f"bank{i}", name=f"bank{i}")
+
+        slot_list = keep.tile([P, S // 16], U16, name="slot_list")
+        pos_lists = [keep.tile([P, T // 16], U16, name=f"pos_list{r}") for r in range(2)]
+        x_tiles = [keep.tile([P, T], I32, name=f"x_tile{o}", align_bytes=64) for o in range(PASSES)]
+        xs_tile = keep.tile([P, T], U8, name="xs_tile", align_bytes=64)
+        bias = keep.tile([P, N // P, E], F32, name="bias")
+        gate_rows = keep.tile([P, P], F32, name="gate_rows")
+        gate_cols = keep.tile([P, 8], F32, name="gate_cols")
+        ident = keep.tile([P, P], F32, name="ident")
+
+        nc.vector.memset(xs_tile[:].bitcast(I32), 0)
+        nc.gpsimd.memset(gate_rows[:], 0.0)
+        make_identity(nc, ident[:])
+
+        nc.sync.dma_start(slot_list[:], offs)
+        for o in range(PASSES):
+            nc.sync.dma_start(out=x_tiles[o][:], in_=x_words[o].rearrange("p t r -> p (t r)").bitcast(I32))
+        for q in range(4):
+            nc.scalar.dma_start(
+                out=xs_tile[32 * q : 32 * q + 4 * PASSES, :].bitcast(I32),
+                in_=x_scales[:, 4 * q : 4 * q + 4, :].bitcast(I32),
+            )
+
+        units = [(h, e, o) for h in range(2) for e in range(E) for o in range(PASSES)]
+        raw = {}
+
+        def load_w(u):
+            h, e, o = units[u]
+            raw[u] = keep.tile([P, PACK, HALF], F32, tag=f"raw{u}", name=f"raw{u}", align_bytes=64)
+            nc.sync.dma_start(
+                out=raw[u][:],
+                in_=w[e, o * KP : (o + 1) * KP, h * HALF : (h + 1) * HALF].rearrange("(p j) n -> p j n", j=PACK),
+            )
+
+        small = [
+            lambda: nc.sync.dma_start(out=bias[:], in_=b.rearrange("(c p) e -> p c e", p=P)),
+            lambda: nc.sync.dma_start(pos_lists[0][:], pos1),
+            lambda: nc.sync.dma_start(pos_lists[1][:], pos2),
+            lambda: nc.sync.dma_start(out=gate_rows[0:4, :], in_=gate[0, 0, :].rearrange("(c p) -> c p", p=P)),
+            lambda: nc.sync.dma_start(out=gate_rows[4:8, :], in_=gate[1, 0, :].rearrange("(c p) -> c p", p=P)),
+        ]
+        for u in range(len(units)):
+            load_w(u)
+            if 2 <= u < 2 + len(small):
+                small[u - 2]()
+        wp_raw = keep.tile([P, PACK, M], F32, name="wp_raw")
+        nc.sync.dma_start(out=wp_raw[:], in_=wp.rearrange("(p j) f -> p j f", j=PACK))
+
+        xg, xsg = {}, {}
+
+        def gather_tokens(i):
+            e, o = divmod(i, PASSES + 1)
+            tag = f"free{i}" if i < FREE_GATHERS else f"raw{i - FREE_GATHERS}"
+            cols = slot_list[:, e * C // 16 : (e + 1) * C // 16]
+            if o < PASSES:
+                xg[o, e] = keep.tile([P, C], U32, tag=tag, name=f"xg{o}_{e}", align_bytes=64)
+                nc.vector.tensor_copy(xg[o, e][:], x_tiles[o][:].bitcast(U32).indirect(cols))
+            else:
+                xsg[e] = keep.tile([P, C], U8, tag=tag, name=f"xsg{e}", align_bytes=64)
+                nc.vector.tensor_copy(xsg[e][:], xs_tile[:].indirect(cols))
+
+        for i in range(FREE_GATHERS):
+            gather_tokens(i)
+
+        def cast(src, width, on_vector, name):
+            grouped = ring.tile([P, width, PACK], BF16, tag="grouped", name=f"grouped{name}", align_bytes=64)
+            view = src.rearrange("p j n -> p n j")
+            if on_vector:
+                nc.vector.tensor_copy(out=grouped[:], in_=view)
+            else:
+                nc.scalar.copy(out=grouped[:], in_=view)
+            return grouped
+
+        def quantize(grouped, width, name):
+            codes = keep.tile([P, width], U32, name=f"codes_{name}", align_bytes=64)
+            scales = keep.tile([P, width], U8, name=f"scales_{name}", align_bytes=64)
+            nc.vector.quantize_mx(
+                out=codes[:].bitcast(FP8X4), scales=scales[:], in_=grouped[:].rearrange("p n j -> p (n j)")
+            )
+            return codes, scales
+
+        y = {}
+        ct = [keep.tile([P, 2, P, 2], BF16, name=f"ct{c}", align_bytes=64) for c in range(T // P)]
+
+        def experts(h):
+            mine = [u for u in range(len(units)) if units[u][0] == h]
+            grouped = {u: cast(raw[u][:], HALF, u in VECTOR_CASTS, u) for u in mine}
+            quantized = {u: quantize(grouped[u], HALF, f"w{u}") for u in mine}
+            if h == 0:
+                for i in range(FREE_GATHERS, E * (PASSES + 1)):
+                    gather_tokens(i)
+                gate_turned = bank(7, [P, P])
+                nc.tensor.transpose(gate_turned[:], gate_rows[:], ident[:])
+                nc.scalar.copy(out=gate_cols[:], in_=gate_turned[:, 0:8])
+            for blk in (2 * h, 2 * h + 1):
+                y[blk] = keep.tile([P, S], F32, tag=f"raw{Y_AFTER[blk]}", name=f"y{blk}", align_bytes=64)
+            for e in range(E):
+                first_bank = 2 * e if h == 0 else 4 + 2 * (e % 2)
+                acc = [bank(first_bank + bl, [P, C]) for bl in range(2)]
+                for o in range(PASSES):
+                    codes, scales = quantized[units.index((h, e, o))]
+                    for bl in range(2):
+                        nc.tensor.matmul_mx(
+                            out=acc[bl][:],
+                            lhsT=codes[:, bl * P : (bl + 1) * P].bitcast(FP8X4),
+                            lhsT_scale=scales[:, bl * P : (bl + 1) * P],
+                            rhs=xg[o, e][:].bitcast(FP8X4),
+                            rhs_scale=xsg[e][4 * o :, :],
+                            start=(o == 0),
+                            stop=(o == PASSES - 1),
+                        )
+                for bl in range(2):
+                    blk = 2 * h + bl
+                    nc.scalar.activation(
+                        out=y[blk][:, e * C : (e + 1) * C], in_=acc[bl][:], func=ACT.Identity, bias=bias[:, blk, e : e + 1]
+                    )
+
+        def combine(h, th, firsts):
+            turned = [bank(2 * th + r, [P, 2, HALF]) for r in range(2)]
+            for r in range(2):
+                after = PICK_AFTER[2 * th + r] if h == 0 else None
+                tag = f"picked{h}{th}{r}" if after is None else f"raw{after}"
+                picked = keep.tile([P, 2, 2 * P], F32, tag=tag, name=f"picked{h}{th}{r}", align_bytes=64)
+                for bl in range(2):
+                    nc.vector.tensor_copy(
+                        picked[:, bl, :], y[2 * h + bl][:].indirect(pos_lists[r][:, th * 16 : (th + 1) * 16])
+                    )
+                    for ci in range(2):
+                        nc.tensor.transpose(
+                            turned[r][:, ci, bl * P : (bl + 1) * P], picked[:, bl, ci * P : (ci + 1) * P], ident[:]
+                        )
+            for ci in range(2):
+                c = 2 * th + ci
+                first = firsts[:, c]
+                nc.scalar.activation(
+                    out=first,
+                    in_=turned[0][:, ci, :].rearrange("t (q u e) -> t u q e", u=2, e=2),
+                    func=ACT.Copy,
+                    scale=gate_cols[:, c : c + 1],
+                )
+                second = turned[1][:, ci, :].rearrange("t (q u e) -> t u q e", u=2, e=2)
+                for u in range(2):
+                    nc.vector.scalar_tensor_tensor(
+                        out=ct[c][:, u, 64 * h : 64 * (h + 1), :],
+                        in0=second[:, u],
+                        scalar=gate_cols[:, 4 + c : 5 + c],
+                        in1=first[:, u],
+                        op0=ALU.mult,
+                        op1=ALU.add,
+                    )
+
+        def project(th, wp_codes, wp_scales):
+            back = bank(4 + th, [P, 2, 2, P])
+            for ci in range(2):
+                words = ct[2 * th + ci][:].rearrange("t u p e -> t (u p e)").bitcast(F32)
+                for u in range(2):
+                    nc.tensor.transpose(back[:, ci, u, :], words[:, u * P : (u + 1) * P], ident[:])
+            c_grouped = keep.tile([P, 2 * P * PACK], BF16, name=f"c_grouped{th}", align_bytes=64)
+            nc.scalar.copy(
+                out=c_grouped[:].bitcast(F32).rearrange("p (c t u) -> p c t u", c=2, u=2),
+                in_=back[:].rearrange("p c u t -> p c t u"),
+            )
+            c_codes = keep.tile([P, 2 * P], U32, name=f"c_codes{th}", align_bytes=64)
+            c_scales = keep.tile([P, 2 * P], U8, name=f"c_scales{th}", align_bytes=64)
+            nc.vector.quantize_mx(out=c_codes[:].bitcast(FP8X4), scales=c_scales[:], in_=c_grouped[:])
+            for fp in range(2):
+                res = bank((6 if th == 0 else 0) + fp, [P, 2, 2 * P])
+                for fi in range(2):
+                    fb = 2 * fp + fi
+                    nc.tensor.matmul_mx(
+                        out=res[:, fi, :],
+                        lhsT=wp_codes[:, fb * P : (fb + 1) * P].bitcast(FP8X4),
+                        lhsT_scale=wp_scales[:, fb * P : (fb + 1) * P],
+                        rhs=c_codes[:].bitcast(FP8X4),
+                        rhs_scale=c_scales[:],
+                        start=True,
+                        stop=True,
+                    )
+                staged = keep.tile([P, 2, 2 * P], F32, name=f"staged{th}{fp}")
+                if fp == 0:
+                    nc.scalar.copy(out=staged[:], in_=res[:])
+                else:
+                    nc.vector.tensor_copy(out=staged[:], in_=res[:])
+                nc.sync.dma_start(
+                    out=out[fp * 2 * P : (fp + 1) * 2 * P, th * 2 * P : (th + 1) * 2 * P].rearrange(
+                        "(i p) t -> p i t", p=P
+                    ),
+                    in_=staged[:],
+                )
+
+        experts(0)
+        experts(1)
+        for h in range(2):
+            tag = f"raw{FIRST_AFTER}" if h == 0 else "firsts"
+            firsts = keep.tile([P, T // P, 2, 64, 2], F32, tag=tag, name=f"firsts{h}", align_bytes=64)
+            for th in range(2):
+                combine(h, th, firsts)
+        wp_codes, wp_scales = quantize(cast(wp_raw[:], M, False, "wp"), M, "wp")
+        for th in range(2):
+            project(th, wp_codes, wp_scales)

@@ -22,7 +22,7 @@ PACK = 4
 KP = P * PACK
 PASSES = K // KP
 HALF = N // 2
-VECTOR_CASTS = (11, 21, 22, 23)
+VECTOR_CASTS = (4, 8, 11, 15, 20, 21, 22, 23)
 FREE_GATHERS = 7
 Y_AFTER = (9, 10, 17, 18)
 PICK_AFTER = (None, 14, 16, 19)
@@ -89,9 +89,16 @@ def tile_moe_nxt_lin_bias_kernel(
         nc.sync.dma_start(out=wp_raw[:], in_=wp.rearrange("(p j) f -> p j f", j=PACK))
 
         xg, xsg = {}, {}
+        token_gathers = [
+            (e, o)
+            for pair in range(0, E, 2)
+            for passes in (range(PASSES), (PASSES,))
+            for e in (pair, pair + 1)
+            for o in passes
+        ]
 
         def gather_tokens(i):
-            e, o = divmod(i, PASSES + 1)
+            e, o = token_gathers[i]
             tag = f"free{i}" if i < FREE_GATHERS else f"raw{i - FREE_GATHERS}"
             cols = slot_list[:, e * C // 16 : (e + 1) * C // 16]
             if o < PASSES:
@@ -106,11 +113,12 @@ def tile_moe_nxt_lin_bias_kernel(
 
         def cast(src, width, on_vector, name):
             grouped = ring.tile([P, width, PACK], BF16, tag="grouped", name=f"grouped{name}", align_bytes=64)
-            view = src.rearrange("p j n -> p n j")
+            view = src.rearrange("p j (c i) -> p c j i", i=4)
+            dst = grouped[:].rearrange("p (c i) j -> p c j i", i=4)
             if on_vector:
-                nc.vector.tensor_copy(out=grouped[:], in_=view)
+                nc.vector.tensor_copy(out=dst, in_=view)
             else:
-                nc.scalar.copy(out=grouped[:], in_=view)
+                nc.scalar.copy(out=dst, in_=view)
             return grouped
 
         def quantize(grouped, width, name):

@@ -22,11 +22,12 @@ PACK = 4
 KP = P * PACK
 PASSES = K // KP
 HALF = N // 2
-VECTOR_CASTS = (4, 8, 11, 15, 20, 21, 22, 23)
-FREE_GATHERS = 7
-Y_AFTER = (9, 10, 17, 18)
-PICK_AFTER = (None, 14, 16, 19)
-FIRST_AFTER = 22
+VECTOR_CASTS = (5, 8, 11, 12, 13, 14, 17, 22, 23)
+FREE_GATHERS = 8
+TIE0 = 0
+Y_AFTER = (9, 10, 19, 20)
+PICK_AFTER = (None, None, None, None)
+FIRST_AFTER = 23
 
 
 def tile_moe_nxt_lin_bias_kernel(
@@ -55,13 +56,8 @@ def tile_moe_nxt_lin_bias_kernel(
         make_identity(nc, ident[:])
 
         nc.sync.dma_start(slot_list[:], offs)
-        for o in range(PASSES):
-            nc.sync.dma_start(out=x_tiles[o][:], in_=x_words[o].rearrange("p t r -> p (t r)").bitcast(I32))
-        for q in range(4):
-            nc.scalar.dma_start(
-                out=xs_tile[32 * q : 32 * q + 4 * PASSES, :].bitcast(I32),
-                in_=x_scales[:, 4 * q : 4 * q + 4, :].bitcast(I32),
-            )
+        for r in range(2):
+            nc.scalar.dma_start(out=gate_rows[4 * r : 4 * r + 4, :], in_=gate[r, 0, :].rearrange("(c p) -> c p", p=P))
 
         units = [(h, e, o) for h in range(2) for e in range(E) for o in range(PASSES)]
         raw = {}
@@ -78,14 +74,20 @@ def tile_moe_nxt_lin_bias_kernel(
             lambda: nc.sync.dma_start(out=bias[:], in_=b.rearrange("(c p) e -> p c e", p=P)),
             lambda: nc.sync.dma_start(pos_lists[0][:], pos1),
             lambda: nc.sync.dma_start(pos_lists[1][:], pos2),
-            lambda: nc.sync.dma_start(out=gate_rows[0:4, :], in_=gate[0, 0, :].rearrange("(c p) -> c p", p=P)),
-            lambda: nc.sync.dma_start(out=gate_rows[4:8, :], in_=gate[1, 0, :].rearrange("(c p) -> c p", p=P)),
         ]
-        for u in range(len(units)):
+        for o in range(PASSES):
+            load_w(o)
+            nc.sync.dma_start(out=x_tiles[o][:], in_=x_words[o].rearrange("p t r -> p (t r)").bitcast(I32))
+        for q in range(4):
+            nc.sync.dma_start(
+                out=xs_tile[32 * q : 32 * q + 4 * PASSES, :].bitcast(I32),
+                in_=x_scales[:, 4 * q : 4 * q + 4, :].bitcast(I32),
+            )
+        for u in range(PASSES, len(units)):
             load_w(u)
-            if 2 <= u < 2 + len(small):
-                small[u - 2]()
-        wp_raw = keep.tile([P, PACK, M], F32, name="wp_raw")
+            if 4 <= u < 4 + len(small):
+                small[u - 4]()
+        wp_raw = keep.tile([P, PACK, M], F32, tag="wp_raw", name="wp_raw", align_bytes=64)
         nc.sync.dma_start(out=wp_raw[:], in_=wp.rearrange("(p j) f -> p j f", j=PACK))
 
         xg, xsg = {}, {}
@@ -99,7 +101,7 @@ def tile_moe_nxt_lin_bias_kernel(
 
         def gather_tokens(i):
             e, o = token_gathers[i]
-            tag = f"free{i}" if i < FREE_GATHERS else f"raw{i - FREE_GATHERS}"
+            tag = f"free{i}" if i < FREE_GATHERS else f"raw{i - FREE_GATHERS + TIE0}"
             cols = slot_list[:, e * C // 16 : (e + 1) * C // 16]
             if o < PASSES:
                 xg[o, e] = keep.tile([P, C], U32, tag=tag, name=f"xg{o}_{e}", align_bytes=64)
@@ -143,7 +145,7 @@ def tile_moe_nxt_lin_bias_kernel(
                 nc.tensor.transpose(gate_turned[:], gate_rows[:], ident[:])
                 nc.scalar.copy(out=gate_cols[:], in_=gate_turned[:, 0:8])
             for blk in (2 * h, 2 * h + 1):
-                y[blk] = keep.tile([P, S], F32, tag=f"raw{Y_AFTER[blk]}", name=f"y{blk}", align_bytes=64)
+                y[blk] = keep.tile([P, S], F32, tag=f"raw{Y_AFTER[blk]}" if Y_AFTER[blk] else f"y{blk}", name=f"y{blk}", align_bytes=64)
             for e in range(E):
                 first_bank = 2 * e if h == 0 else 4 + 2 * (e % 2)
                 acc = [bank(first_bank + bl, [P, C]) for bl in range(2)]
@@ -161,9 +163,11 @@ def tile_moe_nxt_lin_bias_kernel(
                         )
                 for bl in range(2):
                     blk = 2 * h + bl
-                    nc.scalar.activation(
-                        out=y[blk][:, e * C : (e + 1) * C], in_=acc[bl][:], func=ACT.Identity, bias=bias[:, blk, e : e + 1]
-                    )
+                    dst = y[blk][:, e * C : (e + 1) * C]
+                    if e == E - 1 and h == 1 and bl == 0:
+                        nc.vector.tensor_scalar(dst, acc[bl][:], bias[:, blk, e : e + 1], None, ALU.add)
+                    else:
+                        nc.scalar.activation(out=dst, in_=acc[bl][:], func=ACT.Identity, bias=bias[:, blk, e : e + 1])
 
         def combine(h, th, firsts):
             turned = [bank(2 * th + r, [P, 2, HALF]) for r in range(2)]
@@ -240,11 +244,11 @@ def tile_moe_nxt_lin_bias_kernel(
 
         experts(0)
         experts(1)
+        wp_codes, wp_scales = quantize(cast(wp_raw[:], M, False, "wp"), M, "wp")
         for h in range(2):
-            tag = f"raw{FIRST_AFTER}" if h == 0 else "firsts"
+            tag = f"raw{FIRST_AFTER}" if h == 0 else "wp_raw"
             firsts = keep.tile([P, T // P, 2, 64, 2], F32, tag=tag, name=f"firsts{h}", align_bytes=64)
             for th in range(2):
                 combine(h, th, firsts)
-        wp_codes, wp_scales = quantize(cast(wp_raw[:], M, False, "wp"), M, "wp")
         for th in range(2):
             project(th, wp_codes, wp_scales)

@@ -22,12 +22,13 @@ PACK = 4
 KP = P * PACK
 PASSES = K // KP
 HALF = N // 2
-VECTOR_CASTS = (5, 8, 11, 12, 13, 14, 17, 22, 23)
-FREE_GATHERS = 8
-TIE0 = 0
+WINDOW = 768
+WHOLE = 0
+VECTOR_CASTS = (8, 11, 12, 13, 17, 22, 23)
 Y_AFTER = (9, 10, 19, 20)
-PICK_AFTER = (None, None, None, None)
+PICK_AFTER = (None, None)
 FIRST_AFTER = 23
+GROUP_BANKS = (0, 2, 4, 6, 0, 2, 0, 2)
 
 
 def tile_moe_nxt_lin_bias_kernel(
@@ -36,7 +37,7 @@ def tile_moe_nxt_lin_bias_kernel(
     nc = tc.nc
     with ExitStack() as ctx:
         keep = ctx.enter_context(tc.tile_pool(name="keep", bufs=1))
-        ring = ctx.enter_context(tc.tile_pool(name="ring", bufs=8))
+        ring = ctx.enter_context(tc.tile_pool(name="ring", bufs=6))
         psum = ctx.enter_context(tc.psum_pool(name="psum", bufs=1))
 
         def bank(i, shape):
@@ -44,8 +45,8 @@ def tile_moe_nxt_lin_bias_kernel(
 
         slot_list = keep.tile([P, S // 16], U16, name="slot_list")
         pos_lists = [keep.tile([P, T // 16], U16, name=f"pos_list{r}") for r in range(2)]
-        x_tiles = [keep.tile([P, T], I32, name=f"x_tile{o}", align_bytes=64) for o in range(PASSES)]
-        xs_tile = keep.tile([P, T], U8, name="xs_tile", align_bytes=64)
+        x_tiles = [keep.tile([P, WINDOW], I32, name=f"x_tile{o}", align_bytes=64) for o in range(PASSES)]
+        xs_tile = keep.tile([P, WINDOW], U8, name="xs_tile", align_bytes=64)
         bias = keep.tile([P, N // P, E], F32, name="bias")
         gate_rows = keep.tile([P, P], F32, name="gate_rows")
         gate_cols = keep.tile([P, 8], F32, name="gate_cols")
@@ -53,21 +54,25 @@ def tile_moe_nxt_lin_bias_kernel(
 
         nc.vector.memset(xs_tile[:].bitcast(I32), 0)
         nc.gpsimd.memset(gate_rows[:], 0.0)
+        for o in range(PASSES):
+            nc.gpsimd.memset(x_tiles[o][:, T:], 0)
         make_identity(nc, ident[:])
 
         nc.sync.dma_start(slot_list[:], offs)
         for r in range(2):
             nc.scalar.dma_start(out=gate_rows[4 * r : 4 * r + 4, :], in_=gate[r, 0, :].rearrange("(c p) -> c p", p=P))
 
-        units = [(h, e, o) for h in range(2) for e in range(E) for o in range(PASSES)]
+        groups = [(e, range(4)) for e in range(WHOLE)]
+        groups = groups + [(e, range(2 * h, 2 * h + 2)) for h in range(2) for e in range(WHOLE, E)]
+        units = [(e, blocks, o) for e, blocks in groups for o in range(PASSES)]
         raw = {}
 
         def load_w(u):
-            h, e, o = units[u]
-            raw[u] = keep.tile([P, PACK, HALF], F32, tag=f"raw{u}", name=f"raw{u}", align_bytes=64)
+            e, blocks, o = units[u]
+            raw[u] = keep.tile([P, PACK, len(blocks) * P], F32, tag=f"raw{u}", name=f"raw{u}", align_bytes=64)
             nc.sync.dma_start(
                 out=raw[u][:],
-                in_=w[e, o * KP : (o + 1) * KP, h * HALF : (h + 1) * HALF].rearrange("(p j) n -> p j n", j=PACK),
+                in_=w[e, o * KP : (o + 1) * KP, blocks.start * P : blocks.stop * P].rearrange("(p j) n -> p j n", j=PACK),
             )
 
         small = [
@@ -76,11 +81,11 @@ def tile_moe_nxt_lin_bias_kernel(
             lambda: nc.sync.dma_start(pos_lists[1][:], pos2),
         ]
         for o in range(PASSES):
+            nc.sync.dma_start(out=x_tiles[o][:, :T], in_=x_words[o].rearrange("p t r -> p (t r)").bitcast(I32))
             load_w(o)
-            nc.sync.dma_start(out=x_tiles[o][:], in_=x_words[o].rearrange("p t r -> p (t r)").bitcast(I32))
         for q in range(4):
             nc.sync.dma_start(
-                out=xs_tile[32 * q : 32 * q + 4 * PASSES, :].bitcast(I32),
+                out=xs_tile[32 * q : 32 * q + 4 * PASSES, :T].bitcast(I32),
                 in_=x_scales[:, 4 * q : 4 * q + 4, :].bitcast(I32),
             )
         for u in range(PASSES, len(units)):
@@ -90,35 +95,21 @@ def tile_moe_nxt_lin_bias_kernel(
         wp_raw = keep.tile([P, PACK, M], F32, tag="wp_raw", name="wp_raw", align_bytes=64)
         nc.sync.dma_start(out=wp_raw[:], in_=wp.rearrange("(p j) f -> p j f", j=PACK))
 
-        xg, xsg = {}, {}
-        token_gathers = [
-            (e, o)
-            for pair in range(0, E, 2)
-            for passes in (range(PASSES), (PASSES,))
-            for e in (pair, pair + 1)
-            for o in passes
-        ]
-
-        def gather_tokens(i):
-            e, o = token_gathers[i]
-            tag = f"free{i}" if i < FREE_GATHERS else f"raw{i - FREE_GATHERS + TIE0}"
-            cols = slot_list[:, e * C // 16 : (e + 1) * C // 16]
-            if o < PASSES:
-                xg[o, e] = keep.tile([P, C], U32, tag=tag, name=f"xg{o}_{e}", align_bytes=64)
-                nc.vector.tensor_copy(xg[o, e][:], x_tiles[o][:].bitcast(U32).indirect(cols))
-            else:
-                xsg[e] = keep.tile([P, C], U8, tag=tag, name=f"xsg{e}", align_bytes=64)
-                nc.vector.tensor_copy(xsg[e][:], xs_tile[:].indirect(cols))
-
-        for i in range(FREE_GATHERS):
-            gather_tokens(i)
+        xg = [[keep.tile([P, 2 * C], U32, name=f"xg{o}_{i}", align_bytes=64) for i in range(2)] for o in range(PASSES)]
+        xsg = [keep.tile([P, 2 * C], U8, name=f"xsg{i}", align_bytes=64) for i in range(2)]
+        pair_slots = [slot_list[:, i * 2 * C // 16 : (i + 1) * 2 * C // 16] for i in range(2)]
+        for o in range(PASSES):
+            for i in range(2):
+                nc.vector.tensor_copy(xg[o][i][:], x_tiles[o][:].bitcast(U32).indirect(pair_slots[i]))
+        for i in range(2):
+            nc.vector.tensor_copy(xsg[i][:], xs_tile[:].indirect(pair_slots[i]))
 
         def cast(src, width, on_vector, name):
             grouped = ring.tile([P, width, PACK], BF16, tag="grouped", name=f"grouped{name}", align_bytes=64)
             view = src.rearrange("p j (c i) -> p c j i", i=4)
             dst = grouped[:].rearrange("p (c i) j -> p c j i", i=4)
             if on_vector:
-                nc.vector.tensor_copy(out=dst, in_=view)
+                nc.vector.tensor_copy(out=grouped[:], in_=src.rearrange("p j n -> p n j"))
             else:
                 nc.scalar.copy(out=dst, in_=view)
             return grouped
@@ -131,57 +122,62 @@ def tile_moe_nxt_lin_bias_kernel(
             )
             return codes, scales
 
-        y = {}
         ct = [keep.tile([P, 2, P, 2], BF16, name=f"ct{c}", align_bytes=64) for c in range(T // P)]
+        y = {}
 
-        def experts(h):
-            mine = [u for u in range(len(units)) if units[u][0] == h]
-            grouped = {u: cast(raw[u][:], HALF, u in VECTOR_CASTS, u) for u in mine}
-            quantized = {u: quantize(grouped[u], HALF, f"w{u}") for u in mine}
-            if h == 0:
-                for i in range(FREE_GATHERS, E * (PASSES + 1)):
-                    gather_tokens(i)
-                gate_turned = bank(7, [P, P])
-                nc.tensor.transpose(gate_turned[:], gate_rows[:], ident[:])
-                nc.scalar.copy(out=gate_cols[:], in_=gate_turned[:, 0:8])
-            for blk in (2 * h, 2 * h + 1):
-                y[blk] = keep.tile([P, S], F32, tag=f"raw{Y_AFTER[blk]}" if Y_AFTER[blk] else f"y{blk}", name=f"y{blk}", align_bytes=64)
-            for e in range(E):
-                first_bank = 2 * e if h == 0 else 4 + 2 * (e % 2)
-                acc = [bank(first_bank + bl, [P, C]) for bl in range(2)]
+        def experts(which, banks):
+            mine = [u for g in which for u in range(g * PASSES, (g + 1) * PASSES)]
+            pieces = {}
+            for u in mine:
+                width = len(units[u][1]) * P
+                pieces[u] = [cast(raw[u][:], width, u in VECTOR_CASTS, u)]
+            quantized = {}
+            for u in mine:
+                width = len(units[u][1]) * P // len(pieces[u])
+                for i, piece in enumerate(pieces[u]):
+                    codes, scales = quantize(piece, width, f"w{u}_{i}")
+                    for c0 in range(0, width, P):
+                        quantized[u, (i * width + c0) // P] = (codes[:, c0 : c0 + P], scales[:, c0 : c0 + P])
+            if not y:
+                for blk in range(N // P):
+                    y[blk] = keep.tile([P, S], F32, tag=f"raw{Y_AFTER[blk]}" if Y_AFTER[blk] else f"y{blk}", name=f"y{blk}", align_bytes=64)
+            for g in which:
+                e, blocks = groups[g]
+                acc = [bank(banks[g] + bl, [P, C]) for bl in range(len(blocks))]
                 for o in range(PASSES):
-                    codes, scales = quantized[units.index((h, e, o))]
-                    for bl in range(2):
+                    for bl in range(len(blocks)):
+                        codes, scales = quantized[g * PASSES + o, bl]
                         nc.tensor.matmul_mx(
                             out=acc[bl][:],
-                            lhsT=codes[:, bl * P : (bl + 1) * P].bitcast(FP8X4),
-                            lhsT_scale=scales[:, bl * P : (bl + 1) * P],
-                            rhs=xg[o, e][:].bitcast(FP8X4),
-                            rhs_scale=xsg[e][4 * o :, :],
+                            lhsT=codes.bitcast(FP8X4),
+                            lhsT_scale=scales,
+                            rhs=xg[o][e // 2][:, (e % 2) * C : (e % 2 + 1) * C].bitcast(FP8X4),
+                            rhs_scale=xsg[e // 2][4 * o :, (e % 2) * C : (e % 2 + 1) * C],
                             start=(o == 0),
                             stop=(o == PASSES - 1),
                         )
-                for bl in range(2):
-                    blk = 2 * h + bl
+                for bl, blk in enumerate(blocks):
                     dst = y[blk][:, e * C : (e + 1) * C]
-                    if e == E - 1 and h == 1 and bl == 0:
+                    if g == len(groups) - 1 and bl == 0:
                         nc.vector.tensor_scalar(dst, acc[bl][:], bias[:, blk, e : e + 1], None, ALU.add)
                     else:
                         nc.scalar.activation(out=dst, in_=acc[bl][:], func=ACT.Identity, bias=bias[:, blk, e : e + 1])
 
-        def combine(h, th, firsts):
-            turned = [bank(2 * th + r, [P, 2, HALF]) for r in range(2)]
+        def pick(h, r, bl, tokens, tile):
+            nc.vector.tensor_copy(tile, y[2 * h + bl][:].indirect(pos_lists[r][:, tokens.start // 16 : tokens.stop // 16]))
+
+        def combine(h, th, firsts, early):
+            turned = [bank(4 + 2 * th + r, [P, 2, HALF]) for r in range(2)]
             for r in range(2):
-                after = PICK_AFTER[2 * th + r] if h == 0 else None
-                tag = f"picked{h}{th}{r}" if after is None else f"raw{after}"
-                picked = keep.tile([P, 2, 2 * P], F32, tag=tag, name=f"picked{h}{th}{r}", align_bytes=64)
                 for bl in range(2):
-                    nc.vector.tensor_copy(
-                        picked[:, bl, :], y[2 * h + bl][:].indirect(pos_lists[r][:, th * 16 : (th + 1) * 16])
-                    )
+                    if early:
+                        picked = early[r][:, bl, th * 2 * P : (th + 1) * 2 * P]
+                    else:
+                        picked = keep.tile([P, 2 * P], F32, name=f"picked{th}{r}{bl}")[:]
+                        pick(h, r, bl, range(th * 2 * P, (th + 1) * 2 * P), picked)
                     for ci in range(2):
                         nc.tensor.transpose(
-                            turned[r][:, ci, bl * P : (bl + 1) * P], picked[:, bl, ci * P : (ci + 1) * P], ident[:]
+                            turned[r][:, ci, bl * P : (bl + 1) * P], picked[:, ci * P : (ci + 1) * P], ident[:]
                         )
             for ci in range(2):
                 c = 2 * th + ci
@@ -204,7 +200,7 @@ def tile_moe_nxt_lin_bias_kernel(
                     )
 
         def project(th, wp_codes, wp_scales):
-            back = bank(4 + th, [P, 2, 2, P])
+            back = bank(th, [P, 2, 2, P])
             for ci in range(2):
                 words = ct[2 * th + ci][:].rearrange("t u p e -> t (u p e)").bitcast(F32)
                 for u in range(2):
@@ -218,7 +214,7 @@ def tile_moe_nxt_lin_bias_kernel(
             c_scales = keep.tile([P, 2 * P], U8, name=f"c_scales{th}", align_bytes=64)
             nc.vector.quantize_mx(out=c_codes[:].bitcast(FP8X4), scales=c_scales[:], in_=c_grouped[:])
             for fp in range(2):
-                res = bank((6 if th == 0 else 0) + fp, [P, 2, 2 * P])
+                res = bank(2 + 2 * th + fp, [P, 2, 2 * P])
                 for fi in range(2):
                     fb = 2 * fp + fi
                     nc.tensor.matmul_mx(
@@ -242,13 +238,22 @@ def tile_moe_nxt_lin_bias_kernel(
                     in_=staged[:],
                 )
 
-        experts(0)
-        experts(1)
+        gate_turned = bank(7, [P, P])
+        nc.tensor.transpose(gate_turned[:], gate_rows[:], ident[:])
+        nc.scalar.copy(out=gate_cols[:], in_=gate_turned[:, 0:8])
+        experts(range(E), GROUP_BANKS)
+        experts(range(E, len(groups)), GROUP_BANKS)
         wp_codes, wp_scales = quantize(cast(wp_raw[:], M, False, "wp"), M, "wp")
+        early = []
+        for r in range(2):
+            tag = f"raw{PICK_AFTER[r]}" if PICK_AFTER[r] else f"early{r}"
+            early.append(keep.tile([P, 2, T], F32, tag=tag, name=f"early{r}", align_bytes=64))
+            for bl in range(2):
+                pick(0, r, bl, range(T), early[r][:, bl, :])
         for h in range(2):
             tag = f"raw{FIRST_AFTER}" if h == 0 else "wp_raw"
             firsts = keep.tile([P, T // P, 2, 64, 2], F32, tag=tag, name=f"firsts{h}", align_bytes=64)
             for th in range(2):
-                combine(h, th, firsts)
+                combine(h, th, firsts, early if h == 0 else None)
         for th in range(2):
             project(th, wp_codes, wp_scales)

from contextlib import ExitStack

import concourse.mybir as mybir
from concourse.masks import make_identity

K, T, E, C, N, M = 1536, 512, 4, 256, 512, 512
S = E * C
FLOPS = 2 * K * N * S + 2 * N * M * T

F32 = mybir.dt.float32
BF16 = mybir.dt.bfloat16
I32 = mybir.dt.int32
U32 = mybir.dt.uint32
U16 = mybir.dt.uint16
U8 = mybir.dt.uint8
FP8X4 = mybir.dt.float8_e4m3fn_x4
ACT = mybir.ActivationFunctionType
ALU = mybir.AluOpType

P = 128
PACK = 4
KP = P * PACK
PASSES = K // KP
HALF = N // 2
WINDOW = 768
WHOLE = 0
VECTOR_CASTS = (8, 11, 12, 13, 17, 22, 23)
Y_AFTER = (9, 10, 19, 20)
PICK_AFTER = (None, None)
FIRST_AFTER = 23
GROUP_BANKS = (0, 2, 4, 6, 0, 2, 0, 2)


def tile_moe_nxt_lin_bias_kernel(
    tc, x_words, x_scales, w, b, wp, gate, offs, pos1, pos2, out
):
    nc = tc.nc
    with ExitStack() as ctx:
        keep = ctx.enter_context(tc.tile_pool(name="keep", bufs=1))
        ring = ctx.enter_context(tc.tile_pool(name="ring", bufs=6))
        psum = ctx.enter_context(tc.psum_pool(name="psum", bufs=1))

        def bank(i, shape):
            return psum.tile(shape, F32, tag=f"bank{i}", name=f"bank{i}")

        slot_list = keep.tile([P, S // 16], U16, name="slot_list")
        pos_lists = [keep.tile([P, T // 16], U16, name=f"pos_list{r}") for r in range(2)]
        x_tiles = [keep.tile([P, WINDOW], I32, name=f"x_tile{o}", align_bytes=64) for o in range(PASSES)]
        xs_tile = keep.tile([P, WINDOW], U8, name="xs_tile", align_bytes=64)
        bias = keep.tile([P, N // P, E], F32, name="bias")
        gate_rows = keep.tile([P, P], F32, name="gate_rows")
        gate_cols = keep.tile([P, 8], F32, name="gate_cols")
        ident = keep.tile([P, P], F32, name="ident")

        nc.vector.memset(xs_tile[:].bitcast(I32), 0)
        nc.gpsimd.memset(gate_rows[:], 0.0)
        for o in range(PASSES):
            nc.gpsimd.memset(x_tiles[o][:, T:], 0)
        make_identity(nc, ident[:])

        nc.sync.dma_start(slot_list[:], offs)
        for r in range(2):
            nc.scalar.dma_start(out=gate_rows[4 * r : 4 * r + 4, :], in_=gate[r, 0, :].rearrange("(c p) -> c p", p=P))

        groups = [(e, range(4)) for e in range(WHOLE)]
        groups = groups + [(e, range(2 * h, 2 * h + 2)) for h in range(2) for e in range(WHOLE, E)]
        units = [(e, blocks, o) for e, blocks in groups for o in range(PASSES)]
        raw = {}

        def load_w(u):
            e, blocks, o = units[u]
            raw[u] = keep.tile([P, PACK, len(blocks) * P], F32, tag=f"raw{u}", name=f"raw{u}", align_bytes=64)
            nc.sync.dma_start(
                out=raw[u][:],
                in_=w[e, o * KP : (o + 1) * KP, blocks.start * P : blocks.stop * P].rearrange("(p j) n -> p j n", j=PACK),
            )

        small = [
            lambda: nc.sync.dma_start(out=bias[:], in_=b.rearrange("(c p) e -> p c e", p=P)),
            lambda: nc.sync.dma_start(pos_lists[0][:], pos1),
            lambda: nc.sync.dma_start(pos_lists[1][:], pos2),
        ]
        for o in range(PASSES):
            nc.sync.dma_start(out=x_tiles[o][:, :T], in_=x_words[o].rearrange("p t r -> p (t r)").bitcast(I32))
            load_w(o)
        for q in range(4):
            nc.sync.dma_start(
                out=xs_tile[32 * q : 32 * q + 4 * PASSES, :T].bitcast(I32),
                in_=x_scales[:, 4 * q : 4 * q + 4, :].bitcast(I32),
            )
        for u in range(PASSES, len(units)):
            load_w(u)
            if 4 <= u < 4 + len(small):
                small[u - 4]()
        wp_raw = keep.tile([P, PACK, M], F32, tag="wp_raw", name="wp_raw", align_bytes=64)
        nc.sync.dma_start(out=wp_raw[:], in_=wp.rearrange("(p j) f -> p j f", j=PACK))

        xg = [[keep.tile([P, 2 * C], U32, name=f"xg{o}_{i}", align_bytes=64) for i in range(2)] for o in range(PASSES)]
        xsg = [keep.tile([P, 2 * C], U8, name=f"xsg{i}", align_bytes=64) for i in range(2)]
        pair_slots = [slot_list[:, i * 2 * C // 16 : (i + 1) * 2 * C // 16] for i in range(2)]
        for o in range(PASSES):
            for i in range(2):
                nc.vector.tensor_copy(xg[o][i][:], x_tiles[o][:].bitcast(U32).indirect(pair_slots[i]))
        for i in range(2):
            nc.vector.tensor_copy(xsg[i][:], xs_tile[:].indirect(pair_slots[i]))

        def cast(src, width, on_vector, name):
            grouped = ring.tile([P, width, PACK], BF16, tag="grouped", name=f"grouped{name}", align_bytes=64)
            view = src.rearrange("p j (c i) -> p c j i", i=4)
            dst = grouped[:].rearrange("p (c i) j -> p c j i", i=4)
            if on_vector:
                nc.vector.tensor_copy(out=grouped[:], in_=src.rearrange("p j n -> p n j"))
            else:
                nc.scalar.copy(out=dst, in_=view)
            return grouped

        def quantize(grouped, width, name):
            codes = keep.tile([P, width], U32, name=f"codes_{name}", align_bytes=64)
            scales = keep.tile([P, width], U8, name=f"scales_{name}", align_bytes=64)
            nc.vector.quantize_mx(
                out=codes[:].bitcast(FP8X4), scales=scales[:], in_=grouped[:].rearrange("p n j -> p (n j)")
            )
            return codes, scales

        ct = [keep.tile([P, 2, P, 2], BF16, name=f"ct{c}", align_bytes=64) for c in range(T // P)]
        y = {}

        def experts(which, banks):
            mine = [u for g in which for u in range(g * PASSES, (g + 1) * PASSES)]
            pieces = {}
            for u in mine:
                width = len(units[u][1]) * P
                pieces[u] = [cast(raw[u][:], width, u in VECTOR_CASTS, u)]
            quantized = {}
            for u in mine:
                width = len(units[u][1]) * P // len(pieces[u])
                for i, piece in enumerate(pieces[u]):
                    codes, scales = quantize(piece, width, f"w{u}_{i}")
                    for c0 in range(0, width, P):
                        quantized[u, (i * width + c0) // P] = (codes[:, c0 : c0 + P], scales[:, c0 : c0 + P])
            if not y:
                for blk in range(N // P):
                    y[blk] = keep.tile([P, S], F32, tag=f"raw{Y_AFTER[blk]}" if Y_AFTER[blk] else f"y{blk}", name=f"y{blk}", align_bytes=64)
            for g in which:
                e, blocks = groups[g]
                acc = [bank(banks[g] + bl, [P, C]) for bl in range(len(blocks))]
                for o in range(PASSES):
                    for bl in range(len(blocks)):
                        codes, scales = quantized[g * PASSES + o, bl]
                        nc.tensor.matmul_mx(
                            out=acc[bl][:],
                            lhsT=codes.bitcast(FP8X4),
                            lhsT_scale=scales,
                            rhs=xg[o][e // 2][:, (e % 2) * C : (e % 2 + 1) * C].bitcast(FP8X4),
                            rhs_scale=xsg[e // 2][4 * o :, (e % 2) * C : (e % 2 + 1) * C],
                            start=(o == 0),
                            stop=(o == PASSES - 1),
                        )
                for bl, blk in enumerate(blocks):
                    dst = y[blk][:, e * C : (e + 1) * C]
                    if g == len(groups) - 1 and bl == 0:
                        nc.vector.tensor_scalar(dst, acc[bl][:], bias[:, blk, e : e + 1], None, ALU.add)
                    else:
                        nc.scalar.activation(out=dst, in_=acc[bl][:], func=ACT.Identity, bias=bias[:, blk, e : e + 1])

        def pick(h, r, bl, tokens, tile):
            nc.vector.tensor_copy(tile, y[2 * h + bl][:].indirect(pos_lists[r][:, tokens.start // 16 : tokens.stop // 16]))

        def combine(h, th, firsts, early):
            turned = [bank(4 + 2 * th + r, [P, 2, HALF]) for r in range(2)]
            for r in range(2):
                for bl in range(2):
                    if early:
                        picked = early[r][:, bl, th * 2 * P : (th + 1) * 2 * P]
                    else:
                        picked = keep.tile([P, 2 * P], F32, name=f"picked{th}{r}{bl}")[:]
                        pick(h, r, bl, range(th * 2 * P, (th + 1) * 2 * P), picked)
                    for ci in range(2):
                        nc.tensor.transpose(
                            turned[r][:, ci, bl * P : (bl + 1) * P], picked[:, ci * P : (ci + 1) * P], ident[:]
                        )
            for ci in range(2):
                c = 2 * th + ci
                first = firsts[:, c]
                nc.scalar.activation(
                    out=first,
                    in_=turned[0][:, ci, :].rearrange("t (q u e) -> t u q e", u=2, e=2),
                    func=ACT.Copy,
                    scale=gate_cols[:, c : c + 1],
                )
                second = turned[1][:, ci, :].rearrange("t (q u e) -> t u q e", u=2, e=2)
                for u in range(2):
                    nc.vector.scalar_tensor_tensor(
                        out=ct[c][:, u, 64 * h : 64 * (h + 1), :],
                        in0=second[:, u],
                        scalar=gate_cols[:, 4 + c : 5 + c],
                        in1=first[:, u],
                        op0=ALU.mult,
                        op1=ALU.add,
                    )

        def project(th, wp_codes, wp_scales):
            back = bank(th, [P, 2, 2, P])
            for ci in range(2):
                words = ct[2 * th + ci][:].rearrange("t u p e -> t (u p e)").bitcast(F32)
                for u in range(2):
                    nc.tensor.transpose(back[:, ci, u, :], words[:, u * P : (u + 1) * P], ident[:])
            c_grouped = keep.tile([P, 2 * P * PACK], BF16, name=f"c_grouped{th}", align_bytes=64)
            nc.scalar.copy(
                out=c_grouped[:].bitcast(F32).rearrange("p (c t u) -> p c t u", c=2, u=2),
                in_=back[:].rearrange("p c u t -> p c t u"),
            )
            c_codes = keep.tile([P, 2 * P], U32, name=f"c_codes{th}", align_bytes=64)
            c_scales = keep.tile([P, 2 * P], U8, name=f"c_scales{th}", align_bytes=64)
            nc.vector.quantize_mx(out=c_codes[:].bitcast(FP8X4), scales=c_scales[:], in_=c_grouped[:])
            for fp in range(2):
                res = bank(2 + 2 * th + fp, [P, 2, 2 * P])
                for fi in range(2):
                    fb = 2 * fp + fi
                    nc.tensor.matmul_mx(
                        out=res[:, fi, :],
                        lhsT=wp_codes[:, fb * P : (fb + 1) * P].bitcast(FP8X4),
                        lhsT_scale=wp_scales[:, fb * P : (fb + 1) * P],
                        rhs=c_codes[:].bitcast(FP8X4),
                        rhs_scale=c_scales[:],
                        start=True,
                        stop=True,
                    )
                staged = keep.tile([P, 2, 2 * P], F32, name=f"staged{th}{fp}")
                if fp == 0:
                    nc.scalar.copy(out=staged[:], in_=res[:])
                else:
                    nc.vector.tensor_copy(out=staged[:], in_=res[:])
                nc.sync.dma_start(
                    out=out[fp * 2 * P : (fp + 1) * 2 * P, th * 2 * P : (th + 1) * 2 * P].rearrange(
                        "(i p) t -> p i t", p=P
                    ),
                    in_=staged[:],
                )

        gate_turned = bank(7, [P, P])
        nc.tensor.transpose(gate_turned[:], gate_rows[:], ident[:])
        nc.scalar.copy(out=gate_cols[:], in_=gate_turned[:, 0:8])
        experts(range(E), GROUP_BANKS)
        experts(range(E, len(groups)), GROUP_BANKS)
        wp_codes, wp_scales = quantize(cast(wp_raw[:], M, False, "wp"), M, "wp")
        early = []
        for r in range(2):
            tag = f"raw{PICK_AFTER[r]}" if PICK_AFTER[r] else f"early{r}"
            early.append(keep.tile([P, 2, T], F32, tag=tag, name=f"early{r}", align_bytes=64))
            for bl in range(2):
                pick(0, r, bl, range(T), early[r][:, bl, :])
        for h in range(2):
            tag = f"raw{FIRST_AFTER}" if h == 0 else "wp_raw"
            firsts = keep.tile([P, T // P, 2, 64, 2], F32, tag=tag, name=f"firsts{h}", align_bytes=64)
            for th in range(2):
                combine(h, th, firsts, early if h == 0 else None)
        for th in range(2):
            project(th, wp_codes, wp_scales)
